import numpy as np
import ml_dtypes


def mxq(x, axis, fmt="e4m3"):
    dtype, down = {"e4m3": (ml_dtypes.float8_e4m3fn, 7), "e5m2": (ml_dtypes.float8_e5m2, 14)}[fmt]
    v = np.moveaxis(np.asarray(x, np.float32).astype(ml_dtypes.bfloat16).astype(np.float64), axis, -1)
    blocks = v.reshape(v.shape[:-1] + (-1, 32))
    amax = np.abs(blocks).max(-1, keepdims=True)
    byte = np.maximum(np.where(amax > 0, np.frexp(amax)[1] - 1 + 127, 0) - down, 1)
    scale = np.exp2(byte - 127.0)
    codes = (blocks / scale).astype(np.float32).astype(dtype).astype(np.float64)
    return np.moveaxis((codes * scale).reshape(v.shape), -1, axis)


WIDE = False


def mx_kscale(k):
    if not WIDE:
        return np.ones(k)
    levels = np.array([10, -10, 5, -5, 0])
    if k % 512:
        return np.exp2(np.random.permutation(np.resize(levels, k // 32))).repeat(32)
    a = np.empty((k // 512, 16))
    for p in range(k // 512):
        a[p, :8] = np.random.permutation(np.resize(levels, 8))
        for g in range(8):
            far = levels[np.abs(levels - a[p, g]) >= 10]
            a[p, g + 8] = far[np.random.randint(len(far))]
    return np.exp2(a.ravel()).repeat(32)


def f64(x):
    return np.asarray(x).astype(np.float64)


def striped(idx):
    return np.tile(np.asarray(idx).reshape(-1, 16).T, (8, 1)).astype(np.uint16)


def unstriped(offs):
    return offs[:16].T.reshape(-1).astype(np.int64)


E2M1 = np.array([0.0, 0.5, 1.0, 1.5, 2.0, 3.0, 4.0, 6.0, -0.0, -0.5, -1.0, -1.5, -2.0, -3.0, -4.0, -6.0])


def pack_weight(w, fmt):
    k, n = w.shape
    w = f64(np.asarray(w, np.float32).astype(ml_dtypes.bfloat16)).reshape(k // 32, 32, n)
    amax = np.abs(w).max(1)
    if fmt == "e4m3":
        byte = np.frexp(amax)[1] - 1 + 127 - 7
    else:
        mant, ex = np.frexp(amax / 6.0)
        byte = np.where(mant > 0.5, ex, ex - 1) + 127
    byte = np.clip(np.where(amax > 0, byte, 1), 1, 254)
    scaled = (w * np.exp2(127.0 - byte)[:, None, :]).reshape(k, n).astype(np.float32)
    by_word = np.ascontiguousarray(scaled.reshape(k // 512, 128, 4, n).transpose(0, 1, 3, 2))
    if fmt == "e4m3":
        words = by_word.astype(ml_dtypes.float8_e4m3fn).view(np.uint8)
    else:
        c = by_word.astype(ml_dtypes.float4_e2m1fn).view(np.uint8) & 0xF
        words = (c[..., 0::2] | (c[..., 1::2] << 4)).reshape(k // 512, 128, 2 * n)
    return np.ascontiguousarray(words), np.ascontiguousarray(byte.astype(np.uint8).reshape(k // 512, 16, n))


def unpack_weight(words, scales, fmt):
    g, _, n = scales.shape
    words = np.ascontiguousarray(words).reshape(g, 128, n, -1)
    if fmt == "e4m3":
        vals = words.view(ml_dtypes.float8_e4m3fn).astype(np.float64)
    else:
        nib = np.empty((g, 128, n, 4), np.uint8)
        nib[..., 0::2] = words & 0xF
        nib[..., 1::2] = words >> 4
        vals = E2M1[nib]
    vals = vals * np.repeat(np.exp2(scales.astype(np.float64) - 127.0), 8, axis=1)[..., None]
    return vals.transpose(0, 1, 3, 2).reshape(g * 512, n)


def bf(x):
    return np.asarray(x, np.float32).astype(ml_dtypes.bfloat16)


def planes(Y):
    r, m = Y.shape
    b = f64(bf(Y)).reshape(r // 32, 32, m)
    amax = np.abs(b).max(1)
    byte = np.clip(np.where(amax > 0, np.frexp(amax)[1] - 1 + 127 - 7, 1), 1, 254)
    codes = (b * np.exp2(127.0 - byte)[:, None, :]).reshape(r, m).astype(np.float32).astype(ml_dtypes.float8_e4m3fn).view(np.uint8)
    words = codes.reshape(r // 512, 128, 4, m).transpose(0, 1, 3, 2)
    return np.ascontiguousarray(words), np.ascontiguousarray(byte.astype(np.uint8).reshape(r // 512, 16, m))


D, T, I, Q, E = 512, 2048, 512, 256, 512


def setup_inputs():
    n = np.random.standard_normal
    idx = np.random.permutation(T)[:I]
    fd = mx_kscale(D)
    fi = mx_kscale(I)
    ti = np.ones(T)
    ti[idx] = fi
    keysp = pack_weight(n((D, T)) / fd[:, None], "e2m1")
    return {
        "query": (n((D, Q)) * 0.25 / np.sqrt(D) * fd[:, None]).astype(np.float32),
        "keys_words": keysp[0],
        "keys_scales": keysp[1],
        "sharp": np.tile(np.random.uniform(0.3, 2.5, T), (128, 1)).astype(np.float32),
        "tbias": np.tile(0.4 * n(T), (128, 1)).astype(np.float32),
        "size": (np.random.uniform(0.5, 2.0, (1, I)) * fi).astype(np.float32),
        "vals": (n((E, T)) / ti).astype(np.float32),
        "offs": striped(idx),
    }


def reference(query, keys_words, keys_scales, sharp, tbias, size, vals, offs):
    idx = unstriped(offs)
    keysu = unpack_weight(keys_words, keys_scales, "e2m1")
    queryq = mxq(f64(query), 0, "e4m3")
    keysidxg = keysu[:, idx]
    a = queryq.T @ keysidxg
    s = a * f64(sharp)[:1][:, idx] + f64(tbias)[:1][:, idx]
    p = np.exp(s - np.max(s, axis=1, keepdims=True))
    w = p * f64(size) / np.sum(p, axis=1, keepdims=True)
    wt = w.T
    vt = f64(vals)[:, idx].T
    vtq = mxq(vt, 0, "e4m3")
    wtq = mxq(wt, 0, "e4m3")
    o = vtq.T @ wtq
    words, scales = planes(o)
    return o, words, scales

@@ -1,0 +1,202 @@
+from contextlib import ExitStack
+
+import concourse.mybir as mybir
+from concourse.masks import make_identity
+
+D, T, I, Q, E = 512, 2048, 512, 256, 512
+FLOPS = 2 * D * Q * I + 2 * I * E * Q
+BYTES = 4 * D * Q + 2 * 128 * T + 16 * T + 2 * 4 * T + 4 * I + 4 * E * T + 2 * 128 * 32 + 4 * E * Q + E * Q + 16 * Q
+
+F32 = mybir.dt.float32
+BF16 = mybir.dt.bfloat16
+I32 = mybir.dt.int32
+U32 = mybir.dt.uint32
+U16 = mybir.dt.uint16
+U8 = mybir.dt.uint8
+FP8X4 = mybir.dt.float8_e4m3fn_x4
+FP4X4 = mybir.dt.float4_e2m1fn_x4
+ACT = mybir.ActivationFunctionType
+ALU = mybir.AluOpType
+AX = mybir.AxisListType
+
+P = 128
+PACK = 4
+HALVES = Q // P
+
+
+def tile_attend_tokensharpness_pl_kernel(tc, query, keys_words, keys_scales, sharp, tbias, size, vals, offs, out_0, out_1, out_2):
+    nc = tc.nc
+    with ExitStack() as ctx:
+        lists = ctx.enter_context(tc.tile_pool(name="lists", bufs=1))
+        sb = ctx.enter_context(tc.tile_pool(name="sb", bufs=1))
+        ps = ctx.enter_context(tc.psum_pool(name="ps", bufs=1))
+
+        def bank(n, shape, name):
+            return ps.tile(shape, F32, name=name, tag="bank%d" % n)
+
+        def tile(shape, dtype, name, slot=None):
+            return sb.tile(shape, dtype, name=name, tag=slot or name, align_bytes=64)
+
+        offsets = lists.tile([P, I // 16], U16, name="offsets")
+        nc.sync.dma_start(offsets[:], offs)
+
+        ks_pool = tile([P, T], U8, "ks_pool")
+        sharp_pool = tile([P, T], F32, "sharp_pool")
+        tbias_pool = tile([P, T], F32, "tbias_pool")
+        nc.gpsimd.memset(ks_pool[:].bitcast(I32), 0)
+        nc.vector.memset(sharp_pool[0 : P - 1, :], 0.0)
+        nc.vector.memset(tbias_pool[0 : P - 1, :], 0.0)
+        nc.sync.dma_start(sharp_pool[P - 1 : P, :], sharp[0:1, :])
+        nc.sync.dma_start(tbias_pool[P - 1 : P, :], tbias[0:1, :])
+
+        warm_in = tile([P, 1], F32, "warm_in")
+        warm_out = tile([P, 1], F32, "warm_out")
+        nc.gpsimd.memset(warm_in[:], 0.0)
+        nc.scalar.activation(warm_out[:], warm_in[:], ACT.Exp)
+        ident = tile([P, P], F32, "ident")
+        make_identity(nc, ident[:])
+
+        kw_pool = tile([P, T], U16, "kw_pool")
+        nc.sync.dma_start(kw_pool[:].bitcast(I32), keys_words[0].bitcast(I32))
+        q_raw = tile([P, PACK, Q], F32, "q_raw")
+        nc.sync.dma_start(q_raw[:], query.rearrange("(p t) q -> p t q", t=PACK))
+        size_cols = tile([P, PACK], F32, "size_cols")
+        nc.sync.dma_start(size_cols[:], size.rearrange("o (p t) -> (o p) t", t=PACK))
+        for g in range(4):
+            nc.sync.dma_start(ks_pool[32 * g : 32 * g + 4, :].bitcast(I32), keys_scales[0, 4 * g : 4 * g + 4, :].bitcast(I32))
+        vals_planes = vals.rearrange("(m j) t -> j m t", j=PACK)
+        v_pool = [tile([P, T], F32, "v_pool%d" % j) for j in range(PACK)]
+        for j in range(PACK):
+            nc.sync.dma_start(v_pool[j][:], vals_planes[j])
+
+        kw = tile([P, I], U16, "kw")
+        ks = tile([P, I], U8, "ks")
+
+        q_bf = tile([P, Q, PACK], BF16, "q_bf")
+        nc.scalar.copy(q_bf[:].rearrange("p (c i) t -> p c t i", i=4), q_raw[:].rearrange("p t (c i) -> p c t i", i=4))
+        q_codes = tile([P, Q], U32, "q_codes")
+        q_scales = tile([P, Q], U8, "q_scales")
+
+        size_rows = bank(6, [P, PACK, P], "size_rows")
+        for t in range(PACK):
+            nc.tensor.transpose(size_rows[:, t, :], size_cols[:, t : t + 1].to_broadcast([P, P]), ident[:])
+
+        def listed_columns(pool, n, name):
+            row = tile([P, I], F32, name + "_row")
+            nc.vector.tensor_copy(row[:], pool[:].indirect(offsets[:]))
+            turned = bank(n, [P, I // P, P], name + "_turned")
+            for c in range(I // P):
+                nc.tensor.transpose(turned[:, c, :], row[:, P * c : P * (c + 1)], ident[:])
+            cols = tile([P, I // P], F32, name + "_cols")
+            nc.scalar.copy(cols[:], turned[:, :, P - 1])
+            return cols
+
+        sharp_cols = listed_columns(sharp_pool, 4, "sharp")
+        tbias_cols = listed_columns(tbias_pool, 5, "tbias")
+        nc.vector.tensor_copy(kw[:], kw_pool[:].indirect(offsets[:]))
+        nc.vector.tensor_copy(ks[:], ks_pool[:].indirect(offsets[:]))
+        nc.vector.quantize_mx(out=q_codes[:].bitcast(FP8X4), scales=q_scales[:], in_=q_bf[:].rearrange("p q t -> p (q t)"))
+
+        def gather_values(j):
+            picked = tile([P, I], BF16, "v_picked%d" % j)
+            nc.vector.tensor_copy(picked[:], v_pool[j][:].indirect(offsets[:]))
+            return picked
+
+        def turn_words(src, turned):
+            words = src[:].bitcast(F32)
+            for u in range(2):
+                nc.tensor.transpose(turned[:, u, :], words[:, u : 2 * P : 2], ident[:])
+
+        def group_words(grouped, turned):
+            nc.scalar.copy(grouped.rearrange("p x t -> p (x t)").bitcast(F32).rearrange("p (n x u) -> p n x u", x=P, u=2), turned.rearrange("p n u x -> p n x u"))
+
+        def quantize(codes, scales, grouped):
+            nc.vector.quantize_mx(out=codes.bitcast(FP8X4), scales=scales, in_=grouped.rearrange("p x t -> p (x t)"))
+
+        logits_t = []
+        for c in range(I // P):
+            cols = slice(P * c, P * (c + 1))
+            a_t = bank(c, [P, Q], "a_t%d" % c)
+            nc.tensor.matmul_mx(out=a_t[:], lhsT=kw[:, cols].bitcast(FP4X4), lhsT_scale=ks[:, cols], rhs=q_codes[:].bitcast(FP8X4), rhs_scale=q_scales[:], start=True, stop=True)
+            s_t = tile([P, Q], F32, "s_t%d" % c)
+            nc.scalar.activation(s_t[:], a_t[:], ACT.Identity, bias=tbias_cols[:, c : c + 1], scale=sharp_cols[:, c : c + 1])
+            logits_t.append(s_t)
+
+        picked = [gather_values(j) for j in range(2)]
+        logits = [bank(4 + h, [P, I], "logits%d" % h) for h in range(HALVES)]
+        for c in range(I // P):
+            for h in range(HALVES):
+                nc.tensor.transpose(logits[h][:, P * c : P * (c + 1)], logits_t[c][:, P * h : P * (h + 1)], ident[:])
+
+        probs, sums = [], []
+        neg_max = tile([P, HALVES], F32, "neg_max", "v_pool1")
+        for h in range(HALVES):
+            m = neg_max[:, h : h + 1]
+            nc.vector.tensor_reduce(m, logits[h][:], AX.X, ALU.max, negate=True)
+            p = tile([P, I], F32, "probs%d" % h)
+            z = tile([P, 1], F32, "sums%d" % h)
+            nc.scalar.activation(p[:], logits[h][:], ACT.Exp, bias=m, accum_out=z[:])
+            probs.append(p)
+            sums.append(z)
+        picked.append(gather_values(2))
+
+        w_grouped = tile([P, Q, PACK], BF16, "w_grouped")
+        inv_sum = tile([P, HALVES], F32, "inv_sum", "v_pool2")
+        for h in range(HALVES):
+            r = inv_sum[:, h : h + 1]
+            nc.vector.reciprocal(r, sums[h][:])
+            w = tile([P, I], BF16, "w%d" % h)
+            nc.vector.scalar_tensor_tensor(w[:].rearrange("q (p t) -> q p t", t=PACK), probs[h][:].rearrange("q (p t) -> q p t", t=PACK), r, size_rows[:].rearrange("q t p -> q p t"), ALU.mult, ALU.mult)
+            w_turned = bank(h, [P, 1, 2, P], "w_turned%d" % h)
+            turn_words(w, w_turned[:, 0])
+            group_words(w_grouped[:, P * h : P * (h + 1), :], w_turned[:])
+
+        early_turned = bank(7, [P, 2, 2, P], "early_turned")
+        for j in range(2):
+            turn_words(picked[j], early_turned[:, j])
+        early_grouped = tile([P, 2 * P, PACK], BF16, "early_grouped")
+        group_words(early_grouped[:], early_turned[:])
+        early_codes = tile([P, 2 * P], U32, "early_codes", "v_pool2")
+        early_scales = tile([P, 2 * P], U8, "early_scales")
+        quantize(early_codes[:], early_scales[:], early_grouped[:])
+
+        picked.append(gather_values(3))
+        late_codes = tile([P, Q + 2 * P], U32, "late_codes", "v_pool3")
+        late_scales = tile([P, Q + 2 * P], U8, "late_scales")
+        late_grouped = []
+        for j in (2, 3):
+            late_turned = bank(7, [P, 1, 2, P], "late_turned%d" % j)
+            turn_words(picked[j], late_turned[:, 0])
+            grouped = tile([P, P, PACK], BF16, "late_grouped%d" % j)
+            group_words(grouped[:], late_turned[:])
+            late_grouped.append(grouped)
+        quantize(late_codes[:, 0:Q], late_scales[:, 0:Q], w_grouped[:])
+        v_mx = [(early_codes[:, P * j : P * (j + 1)], early_scales[:, P * j : P * (j + 1)]) for j in range(2)]
+        for j in range(2):
+            cols = slice(Q + P * j, Q + P * (j + 1))
+            quantize(late_codes[:, cols], late_scales[:, cols], late_grouped[j][:])
+            v_mx.append((late_codes[:, cols], late_scales[:, cols]))
+
+        y_f32 = tile([P, PACK, Q], F32, "y_f32")
+        out_planes = out_0.rearrange("(m j) q -> m j q", j=PACK)
+        for j, n in enumerate((2, 3, 4, 6)):
+            y = bank(n, [P, Q], "y%d" % j)
+            nc.tensor.matmul_mx(out=y[:], lhsT=v_mx[j][0].bitcast(FP8X4), lhsT_scale=v_mx[j][1], rhs=late_codes[:, 0:Q].bitcast(FP8X4), rhs_scale=late_scales[:, 0:Q], start=True, stop=True)
+            if j == 2:
+                nc.vector.tensor_copy(y_f32[:, j, :], y[:])
+            else:
+                nc.scalar.copy(y_f32[:, j, :], y[:])
+            if j == 1:
+                nc.sync.dma_start(out_planes[:, 0:2, :], y_f32[:, 0:2, :])
+            if j == 3:
+                nc.scalar.dma_start(out_planes[:, 2:4, :], y_f32[:, 2:4, :])
+
+        y_bf = tile([P, Q, PACK], BF16, "y_bf")
+        nc.vector.tensor_copy(y_bf[:].rearrange("m (c i) j -> m c j i", i=4), y_f32[:].rearrange("m j (c i) -> m c j i", i=4))
+        y_codes = tile([P, Q], U32, "y_codes")
+        y_scales = tile([P, Q], U8, "y_scales")
+        quantize(y_codes[:], y_scales[:], y_bf[:])
+        nc.sync.dma_start(out_1[0].rearrange("m q j -> m (q j)").bitcast(I32), y_codes[:].bitcast(I32))
+        for g in range(4):
+            queue = nc.sync if g % 2 == 0 else nc.scalar
+            queue.dma_start(out_2[0, 4 * g : 4 * g + 4, :].bitcast(I32), y_scales[32 * g : 32 * g + 4, :].bitcast(I32))

@@ -29,6 +29,7 @@ def tile_attend_tokensharpness_pl_kernel(tc, query, keys_words, keys_scales, sha
     with ExitStack() as ctx:
         lists = ctx.enter_context(tc.tile_pool(name="lists", bufs=1))
         sb = ctx.enter_context(tc.tile_pool(name="sb", bufs=1))
+        reused = ctx.enter_context(tc.tile_pool(name="reused", bufs=1))
         ps = ctx.enter_context(tc.psum_pool(name="ps", bufs=1))
 
         def bank(n, shape, name):
@@ -65,7 +66,7 @@ def tile_attend_tokensharpness_pl_kernel(tc, query, keys_words, keys_scales, sha
         for g in range(4):
             nc.sync.dma_start(ks_pool[32 * g : 32 * g + 4, :].bitcast(I32), keys_scales[0, 4 * g : 4 * g + 4, :].bitcast(I32))
         vals_planes = vals.rearrange("(m j) t -> j m t", j=PACK)
-        v_pool = [tile([P, T], F32, "v_pool%d" % j) for j in range(PACK)]
+        v_pool = [tile([P, T], F32, "v_pool%d" % j) if j != 2 else reused.tile([P, T], F32, name="v_pool2", align_bytes=64, offset=0) for j in range(PACK)]
         for j in range(PACK):
             nc.sync.dma_start(v_pool[j][:], vals_planes[j])
 
@@ -113,52 +114,52 @@ def tile_attend_tokensharpness_pl_kernel(tc, query, keys_words, keys_scales, sha
         def quantize(codes, scales, grouped):
             nc.vector.quantize_mx(out=codes.bitcast(FP8X4), scales=scales, in_=grouped.rearrange("p x t -> p (x t)"))
 
-        logits_t = []
-        for c in range(I // P):
-            cols = slice(P * c, P * (c + 1))
-            a_t = bank(c, [P, Q], "a_t%d" % c)
-            nc.tensor.matmul_mx(out=a_t[:], lhsT=kw[:, cols].bitcast(FP4X4), lhsT_scale=ks[:, cols], rhs=q_codes[:].bitcast(FP8X4), rhs_scale=q_scales[:], start=True, stop=True)
-            s_t = tile([P, Q], F32, "s_t%d" % c)
-            nc.scalar.activation(s_t[:], a_t[:], ACT.Identity, bias=tbias_cols[:, c : c + 1], scale=sharp_cols[:, c : c + 1])
-            logits_t.append(s_t)
-
+        halves = [slice(P * h, P * (h + 1)) for h in range(HALVES)]
+        first_scores = [bank(c, [P, P], "first_scores%d" % c) for c in range(I // P)]
+        second_scores = bank(7, [P, I // P, P], "second_scores")
+        scores_t = [[t[:] for t in first_scores], [second_scores[:, c, :] for c in range(I // P)]]
+        for h in range(HALVES):
+            for c in range(I // P):
+                cols = slice(P * c, P * (c + 1))
+                nc.tensor.matmul_mx(out=scores_t[h][c], lhsT=kw[:, cols].bitcast(FP4X4), lhsT_scale=ks[:, cols], rhs=q_codes[:, halves[h]].bitcast(FP8X4), rhs_scale=q_scales[:, halves[h]], start=True, stop=True)
         picked = [gather_values(j) for j in range(2)]
         logits = [bank(4 + h, [P, I], "logits%d" % h) for h in range(HALVES)]
-        for c in range(I // P):
-            for h in range(HALVES):
-                nc.tensor.transpose(logits[h][:, P * c : P * (c + 1)], logits_t[c][:, P * h : P * (h + 1)], ident[:])
+        for h in range(HALVES):
+            for c in range(I // P):
+                s_t = tile([P, P], F32, "s_t%d_%d" % (h, c))
+                nc.scalar.activation(s_t[:], scores_t[h][c], ACT.Identity, bias=tbias_cols[:, c : c + 1], scale=sharp_cols[:, c : c + 1])
+                nc.tensor.transpose(logits[h][:, P * c : P * (c + 1)], s_t[:], ident[:])
 
-        probs, sums = [], []
+        probs = []
+        sums = tile([P, HALVES], F32, "sums")
         neg_max = tile([P, HALVES], F32, "neg_max", "v_pool1")
         for h in range(HALVES):
             m = neg_max[:, h : h + 1]
             nc.vector.tensor_reduce(m, logits[h][:], AX.X, ALU.max, negate=True)
             p = tile([P, I], F32, "probs%d" % h)
-            z = tile([P, 1], F32, "sums%d" % h)
-            nc.scalar.activation(p[:], logits[h][:], ACT.Exp, bias=m, accum_out=z[:])
+            nc.scalar.activation(p[:], logits[h][:], ACT.Exp, bias=m, accum_out=sums[:, h : h + 1])
             probs.append(p)
-            sums.append(z)
         picked.append(gather_values(2))
 
         w_grouped = tile([P, Q, PACK], BF16, "w_grouped")
-        inv_sum = tile([P, HALVES], F32, "inv_sum", "v_pool2")
-        for h in range(HALVES):
-            r = inv_sum[:, h : h + 1]
-            nc.vector.reciprocal(r, sums[h][:])
-            w = tile([P, I], BF16, "w%d" % h)
-            nc.vector.scalar_tensor_tensor(w[:].rearrange("q (p t) -> q p t", t=PACK), probs[h][:].rearrange("q (p t) -> q p t", t=PACK), r, size_rows[:].rearrange("q t p -> q p t"), ALU.mult, ALU.mult)
-            w_turned = bank(h, [P, 1, 2, P], "w_turned%d" % h)
-            turn_words(w, w_turned[:, 0])
-            group_words(w_grouped[:, P * h : P * (h + 1), :], w_turned[:])
-
+        inv_sum = reused.tile([P, HALVES], F32, name="inv_sum", align_bytes=64, offset=0)
+        nc.vector.reciprocal(inv_sum[:], sums[:])
         early_turned = bank(7, [P, 2, 2, P], "early_turned")
         for j in range(2):
             turn_words(picked[j], early_turned[:, j])
         early_grouped = tile([P, 2 * P, PACK], BF16, "early_grouped")
         group_words(early_grouped[:], early_turned[:])
-        early_codes = tile([P, 2 * P], U32, "early_codes", "v_pool2")
+        early_codes = reused.tile([P, 2 * P], U32, name="early_codes", align_bytes=64, offset=64)
         early_scales = tile([P, 2 * P], U8, "early_scales")
         quantize(early_codes[:], early_scales[:], early_grouped[:])
+
+        for h in range(HALVES):
+            r = inv_sum[:, h : h + 1]
+            w = tile([P, I], BF16, "w%d" % h)
+            nc.vector.scalar_tensor_tensor(w[:].rearrange("q (p t) -> q p t", t=PACK), probs[h][:].rearrange("q (p t) -> q p t", t=PACK), r, size_rows[:].rearrange("q t p -> q p t"), ALU.mult, ALU.mult)
+            w_turned = bank(h, [P, 1, 2, P], "w_turned%d" % h)
+            turn_words(w, w_turned[:, 0])
+            group_words(w_grouped[:, P * h : P * (h + 1), :], w_turned[:])
 
         picked.append(gather_values(3))
         late_codes = tile([P, Q + 2 * P], U32, "late_codes", "v_pool3")
@@ -179,23 +180,26 @@ def tile_attend_tokensharpness_pl_kernel(tc, query, keys_words, keys_scales, sha
 
         y_f32 = tile([P, PACK, Q], F32, "y_f32")
         out_planes = out_0.rearrange("(m j) q -> m j q", j=PACK)
-        for j, n in enumerate((2, 3, 4, 6)):
-            y = bank(n, [P, Q], "y%d" % j)
-            nc.tensor.matmul_mx(out=y[:], lhsT=v_mx[j][0].bitcast(FP8X4), lhsT_scale=v_mx[j][1], rhs=late_codes[:, 0:Q].bitcast(FP8X4), rhs_scale=late_scales[:, 0:Q], start=True, stop=True)
-            if j == 2:
-                nc.vector.tensor_copy(y_f32[:, j, :], y[:])
-            else:
-                nc.scalar.copy(y_f32[:, j, :], y[:])
-            if j == 1:
-                nc.sync.dma_start(out_planes[:, 0:2, :], y_f32[:, 0:2, :])
-            if j == 3:
-                nc.scalar.dma_start(out_planes[:, 2:4, :], y_f32[:, 2:4, :])
+        def product(j, n, cols):
+            y = bank(n, [P, cols.stop - cols.start], "y%d" % n)
+            nc.tensor.matmul_mx(out=y[:], lhsT=v_mx[j][0].bitcast(FP8X4), lhsT_scale=v_mx[j][1], rhs=late_codes[:, cols].bitcast(FP8X4), rhs_scale=late_scales[:, cols], start=True, stop=True)
+            return y
 
-        y_bf = tile([P, Q, PACK], BF16, "y_bf")
-        nc.vector.tensor_copy(y_bf[:].rearrange("m (c i) j -> m c j i", i=4), y_f32[:].rearrange("m j (c i) -> m c j i", i=4))
+        nc.scalar.copy(y_f32[:, 0, :], product(0, 2, slice(0, Q))[:])
+        nc.scalar.copy(y_f32[:, 1, :], product(1, 3, slice(0, Q))[:])
+        nc.vector.tensor_copy(y_f32[:, 2, :], product(2, 4, slice(0, Q))[:])
+        nc.sync.dma_start(out_planes[:, 0:3, :], y_f32[:, 0:3, :])
+        nc.scalar.copy(y_f32[:, 3, halves[0]], product(3, 5, halves[0])[:])
+        nc.vector.tensor_copy(y_f32[:, 3, halves[1]], product(3, 6, halves[1])[:])
+        nc.scalar.dma_start(out_planes[:, 3, :], y_f32[:, 3, :])
+
         y_codes = tile([P, Q], U32, "y_codes")
         y_scales = tile([P, Q], U8, "y_scales")
-        quantize(y_codes[:], y_scales[:], y_bf[:])
+        y_bf = [tile([P, P, PACK], BF16, "y_bf%d" % h) for h in range(HALVES)]
+        for h in range(HALVES):
+            nc.vector.tensor_copy(y_bf[h][:].rearrange("m (c i) j -> m c j i", i=4), y_f32[:, :, halves[h]].rearrange("m j (c i) -> m c j i", i=4))
+        for h in range(HALVES):
+            quantize(y_codes[:, halves[h]], y_scales[:, halves[h]], y_bf[h][:])
         nc.sync.dma_start(out_1[0].rearrange("m q j -> m (q j)").bitcast(I32), y_codes[:].bitcast(I32))
         for g in range(4):
             queue = nc.sync if g % 2 == 0 else nc.scalar

@@ -45,17 +45,16 @@ def tile_attend_tokensharpness_pl_kernel(tc, query, keys_words, keys_scales, sha
         sharp_pool = tile([P, T], F32, "sharp_pool")
         tbias_pool = tile([P, T], F32, "tbias_pool")
         nc.gpsimd.memset(ks_pool[:].bitcast(I32), 0)
+        ident = tile([P, P], F32, "ident")
+        nc.vector.memset(ident[:], 0.0)
+        make_identity(nc, ident[:], nomemset=True)
         nc.vector.memset(sharp_pool[0 : P - 1, :], 0.0)
         nc.vector.memset(tbias_pool[0 : P - 1, :], 0.0)
         nc.sync.dma_start(sharp_pool[P - 1 : P, :], sharp[0:1, :])
         nc.sync.dma_start(tbias_pool[P - 1 : P, :], tbias[0:1, :])
 
-        warm_in = tile([P, 1], F32, "warm_in")
-        warm_out = tile([P, 1], F32, "warm_out")
-        nc.gpsimd.memset(warm_in[:], 0.0)
-        nc.scalar.activation(warm_out[:], warm_in[:], ACT.Exp)
-        ident = tile([P, P], F32, "ident")
-        make_identity(nc, ident[:])
+        warm = tile([P, 1], F32, "warm")
+        nc.scalar.activation(warm[:], ident[:, 0:1], ACT.Exp)
 
         kw_pool = tile([P, T], U16, "kw_pool")
         nc.sync.dma_start(kw_pool[:].bitcast(I32), keys_words[0].bitcast(I32))
@@ -78,9 +77,9 @@ def tile_attend_tokensharpness_pl_kernel(tc, query, keys_words, keys_scales, sha
         q_codes = tile([P, Q], U32, "q_codes")
         q_scales = tile([P, Q], U8, "q_scales")
 
-        size_rows = bank(6, [P, PACK, P], "size_rows")
+        size_rows = bank(6, [P, I], "size_rows")
         for t in range(PACK):
-            nc.tensor.transpose(size_rows[:, t, :], size_cols[:, t : t + 1].to_broadcast([P, P]), ident[:])
+            nc.tensor.transpose(size_rows[:, t:I:PACK], size_cols[:, t : t + 1].to_broadcast([P, P]), ident[:])
 
         def listed_columns(pool, n, name):
             row = tile([P, I], F32, name + "_row")
@@ -156,7 +155,7 @@ def tile_attend_tokensharpness_pl_kernel(tc, query, keys_words, keys_scales, sha
         for h in range(HALVES):
             r = inv_sum[:, h : h + 1]
             w = tile([P, I], BF16, "w%d" % h)
-            nc.vector.scalar_tensor_tensor(w[:].rearrange("q (p t) -> q p t", t=PACK), probs[h][:].rearrange("q (p t) -> q p t", t=PACK), r, size_rows[:].rearrange("q t p -> q p t"), ALU.mult, ALU.mult)
+            nc.vector.scalar_tensor_tensor(w[:], probs[h][:], r, size_rows[:], ALU.mult, ALU.mult)
             w_turned = bank(h, [P, 1, 2, P], "w_turned%d" % h)
             turn_words(w, w_turned[:, 0])
             group_words(w_grouped[:, P * h : P * (h + 1), :], w_turned[:])

@@ -5,7 +5,7 @@ from concourse.masks import make_identity
 
 D, T, I, Q, E = 512, 2048, 512, 256, 512
 FLOPS = 2 * D * Q * I + 2 * I * E * Q
-BYTES = 4 * D * Q + 2 * 128 * T + 16 * T + 2 * 4 * T + 4 * I + 4 * E * T + 2 * 128 * 32 + 4 * E * Q + E * Q + 16 * Q
+BYTES = 4 * D * Q + D * T // 2 + D * T // 32 + 2 * 4 * T + 4 * I + 4 * E * T + 2 * 8 * I + 4 * E * Q + E * Q + E * Q // 32
 
 F32 = mybir.dt.float32
 BF16 = mybir.dt.bfloat16
@@ -21,7 +21,11 @@ AX = mybir.AxisListType
 
 P = 128
 PACK = 4
+QUADRANT = 32
+LINE = 4
 HALVES = Q // P
+CHUNKS = I // P
+ROW = P - 1
 
 
 def tile_attend_tokensharpness_pl_kernel(tc, query, keys_words, keys_scales, sharp, tbias, size, vals, offs, out_0, out_1, out_2):
@@ -35,8 +39,11 @@ def tile_attend_tokensharpness_pl_kernel(tc, query, keys_words, keys_scales, sha
         def bank(n, shape, name):
             return ps.tile(shape, F32, name=name, tag="bank%d" % n)
 
-        def tile(shape, dtype, name, slot=None):
-            return sb.tile(shape, dtype, name=name, tag=slot or name, align_bytes=64)
+        def tile(shape, dtype, name, instead_of=None):
+            return sb.tile(shape, dtype, name=name, tag=instead_of or name, align_bytes=64)
+
+        def tile_at(offset, shape, dtype, name):
+            return reused.tile(shape, dtype, name=name, align_bytes=64, offset=offset)
 
         offsets = lists.tile([P, I // 16], U16, name="offsets")
         nc.sync.dma_start(offsets[:], offs)
@@ -48,13 +55,10 @@ def tile_attend_tokensharpness_pl_kernel(tc, query, keys_words, keys_scales, sha
         ident = tile([P, P], F32, "ident")
         nc.vector.memset(ident[:], 0.0)
         make_identity(nc, ident[:], nomemset=True)
-        nc.vector.memset(sharp_pool[0 : P - 1, :], 0.0)
-        nc.vector.memset(tbias_pool[0 : P - 1, :], 0.0)
-        nc.sync.dma_start(sharp_pool[P - 1 : P, :], sharp[0:1, :])
-        nc.sync.dma_start(tbias_pool[P - 1 : P, :], tbias[0:1, :])
-
-        warm = tile([P, 1], F32, "warm")
-        nc.scalar.activation(warm[:], ident[:, 0:1], ACT.Exp)
+        nc.vector.memset(sharp_pool[0:ROW, :], 0.0)
+        nc.vector.memset(tbias_pool[0:ROW, :], 0.0)
+        nc.sync.dma_start(sharp_pool[ROW:P, :], sharp[0:1, :])
+        nc.sync.dma_start(tbias_pool[ROW:P, :], tbias[0:1, :])
 
         kw_pool = tile([P, T], U16, "kw_pool")
         nc.sync.dma_start(kw_pool[:].bitcast(I32), keys_words[0].bitcast(I32))
@@ -62,18 +66,18 @@ def tile_attend_tokensharpness_pl_kernel(tc, query, keys_words, keys_scales, sha
         nc.sync.dma_start(q_raw[:], query.rearrange("(p t) q -> p t q", t=PACK))
         size_cols = tile([P, PACK], F32, "size_cols")
         nc.sync.dma_start(size_cols[:], size.rearrange("o (p t) -> (o p) t", t=PACK))
-        for g in range(4):
-            nc.sync.dma_start(ks_pool[32 * g : 32 * g + 4, :].bitcast(I32), keys_scales[0, 4 * g : 4 * g + 4, :].bitcast(I32))
+        for r in range(4):
+            nc.sync.dma_start(ks_pool[r:P:QUADRANT, :].bitcast(I32), keys_scales[0, r:16:4, :].bitcast(I32))
         vals_planes = vals.rearrange("(m j) t -> j m t", j=PACK)
-        v_pool = [tile([P, T], F32, "v_pool%d" % j) if j != 2 else reused.tile([P, T], F32, name="v_pool2", align_bytes=64, offset=0) for j in range(PACK)]
+        v_pool = [tile_at(0, [P, T], F32, "v_pool2") if j == 2 else tile([P, T], F32, "v_pool%d" % j) for j in range(PACK)]
         for j in range(PACK):
             nc.sync.dma_start(v_pool[j][:], vals_planes[j])
 
         kw = tile([P, I], U16, "kw")
         ks = tile([P, I], U8, "ks")
 
-        q_bf = tile([P, Q, PACK], BF16, "q_bf")
-        nc.scalar.copy(q_bf[:].rearrange("p (c i) t -> p c t i", i=4), q_raw[:].rearrange("p t (c i) -> p c t i", i=4))
+        q_grouped = tile([P, Q, PACK], BF16, "q_grouped")
+        nc.scalar.activation(q_grouped[:].rearrange("p (c i) t -> p c t i", i=LINE), q_raw[:].rearrange("p t (c i) -> p c t i", i=LINE), ACT.Copy)
         q_codes = tile([P, Q], U32, "q_codes")
         q_scales = tile([P, Q], U8, "q_scales")
 
@@ -81,21 +85,15 @@ def tile_attend_tokensharpness_pl_kernel(tc, query, keys_words, keys_scales, sha
         for t in range(PACK):
             nc.tensor.transpose(size_rows[:, t:I:PACK], size_cols[:, t : t + 1].to_broadcast([P, P]), ident[:])
 
-        def listed_columns(pool, n, name):
+        def listed_columns(window, n, name, instead_of=None):
             row = tile([P, I], F32, name + "_row")
-            nc.vector.tensor_copy(row[:], pool[:].indirect(offsets[:]))
-            turned = bank(n, [P, I // P, P], name + "_turned")
-            for c in range(I // P):
+            nc.vector.tensor_copy(row[:], window[:].indirect(offsets[:]))
+            turned = bank(n, [P, CHUNKS, P], name + "_turned")
+            for c in range(CHUNKS):
                 nc.tensor.transpose(turned[:, c, :], row[:, P * c : P * (c + 1)], ident[:])
-            cols = tile([P, I // P], F32, name + "_cols")
-            nc.scalar.copy(cols[:], turned[:, :, P - 1])
+            cols = tile([P, CHUNKS], F32, name + "_cols", instead_of)
+            nc.scalar.activation(cols[:], turned[:, :, ROW], ACT.Copy)
             return cols
-
-        sharp_cols = listed_columns(sharp_pool, 4, "sharp")
-        tbias_cols = listed_columns(tbias_pool, 5, "tbias")
-        nc.vector.tensor_copy(kw[:], kw_pool[:].indirect(offsets[:]))
-        nc.vector.tensor_copy(ks[:], ks_pool[:].indirect(offsets[:]))
-        nc.vector.quantize_mx(out=q_codes[:].bitcast(FP8X4), scales=q_scales[:], in_=q_bf[:].rearrange("p q t -> p (q t)"))
 
         def gather_values(j):
             picked = tile([P, I], BF16, "v_picked%d" % j)
@@ -108,60 +106,74 @@ def tile_attend_tokensharpness_pl_kernel(tc, query, keys_words, keys_scales, sha
                 nc.tensor.transpose(turned[:, u, :], words[:, u : 2 * P : 2], ident[:])
 
         def group_words(grouped, turned):
-            nc.scalar.copy(grouped.rearrange("p x t -> p (x t)").bitcast(F32).rearrange("p (n x u) -> p n x u", x=P, u=2), turned.rearrange("p n u x -> p n x u"))
+            words = grouped.rearrange("p x t -> p (x t)").bitcast(F32)
+            nc.scalar.copy(words.rearrange("p (n x u) -> p n x u", x=P, u=2), turned.rearrange("p n u x -> p n x u"))
 
         def quantize(codes, scales, grouped):
             nc.vector.quantize_mx(out=codes.bitcast(FP8X4), scales=scales, in_=grouped.rearrange("p x t -> p (x t)"))
 
+        sharp_cols = listed_columns(sharp_pool, 4, "sharp", instead_of="q_raw")
+        tbias_cols = listed_columns(tbias_pool, 5, "tbias")
+        nc.vector.tensor_copy(kw[:], kw_pool[:].indirect(offsets[:]))
+        nc.vector.tensor_copy(ks[:], ks_pool[:].indirect(offsets[:]))
+        quantize(q_codes[:], q_scales[:], q_grouped[:])
+
         halves = [slice(P * h, P * (h + 1)) for h in range(HALVES)]
-        first_scores = [bank(c, [P, P], "first_scores%d" % c) for c in range(I // P)]
-        second_scores = bank(7, [P, I // P, P], "second_scores")
-        scores_t = [[t[:] for t in first_scores], [second_scores[:, c, :] for c in range(I // P)]]
+        first_scores = [bank(c, [P, P], "first_scores%d" % c) for c in range(CHUNKS)]
+        second_scores = bank(7, [P, CHUNKS, P], "second_scores")
+        scores = [[first_scores[c][:] for c in range(CHUNKS)], [second_scores[:, c, :] for c in range(CHUNKS)]]
         for h in range(HALVES):
-            for c in range(I // P):
-                cols = slice(P * c, P * (c + 1))
-                nc.tensor.matmul_mx(out=scores_t[h][c], lhsT=kw[:, cols].bitcast(FP4X4), lhsT_scale=ks[:, cols], rhs=q_codes[:, halves[h]].bitcast(FP8X4), rhs_scale=q_scales[:, halves[h]], start=True, stop=True)
+            for c in range(CHUNKS):
+                slots = slice(P * c, P * (c + 1))
+                nc.tensor.matmul_mx(
+                    out=scores[h][c],
+                    lhsT=kw[:, slots].bitcast(FP4X4),
+                    lhsT_scale=ks[:, slots],
+                    rhs=q_codes[:, halves[h]].bitcast(FP8X4),
+                    rhs_scale=q_scales[:, halves[h]],
+                    start=True,
+                    stop=True,
+                )
         picked = [gather_values(j) for j in range(2)]
         logits = [bank(4 + h, [P, I], "logits%d" % h) for h in range(HALVES)]
         for h in range(HALVES):
-            for c in range(I // P):
-                s_t = tile([P, P], F32, "s_t%d_%d" % (h, c))
-                nc.scalar.activation(s_t[:], scores_t[h][c], ACT.Identity, bias=tbias_cols[:, c : c + 1], scale=sharp_cols[:, c : c + 1])
-                nc.tensor.transpose(logits[h][:, P * c : P * (c + 1)], s_t[:], ident[:])
+            for c in range(CHUNKS):
+                by_slot = tile([P, P], F32, "by_slot%d_%d" % (h, c))
+                nc.scalar.activation(by_slot[:], scores[h][c], ACT.Identity, bias=tbias_cols[:, c : c + 1], scale=sharp_cols[:, c : c + 1])
+                nc.tensor.transpose(logits[h][:, P * c : P * (c + 1)], by_slot[:], ident[:])
 
         probs = []
         sums = tile([P, HALVES], F32, "sums")
-        neg_max = tile([P, HALVES], F32, "neg_max", "v_pool1")
+        neg_max = tile([P, HALVES], F32, "neg_max", instead_of="v_pool1")
         for h in range(HALVES):
-            m = neg_max[:, h : h + 1]
-            nc.vector.tensor_reduce(m, logits[h][:], AX.X, ALU.max, negate=True)
-            p = tile([P, I], F32, "probs%d" % h)
-            nc.scalar.activation(p[:], logits[h][:], ACT.Exp, bias=m, accum_out=sums[:, h : h + 1])
-            probs.append(p)
+            nc.vector.tensor_reduce(neg_max[:, h : h + 1], logits[h][:], AX.X, ALU.max, negate=True)
+            prob = tile([P, I], F32, "probs%d" % h)
+            nc.scalar.activation(prob[:], logits[h][:], ACT.Exp, bias=neg_max[:, h : h + 1], accum_out=sums[:, h : h + 1])
+            probs.append(prob)
         picked.append(gather_values(2))
 
         w_grouped = tile([P, Q, PACK], BF16, "w_grouped")
-        inv_sum = reused.tile([P, HALVES], F32, name="inv_sum", align_bytes=64, offset=0)
+        inv_sum = tile_at(0, [P, HALVES], F32, "inv_sum")
         nc.vector.reciprocal(inv_sum[:], sums[:])
+
         early_turned = bank(7, [P, 2, 2, P], "early_turned")
         for j in range(2):
             turn_words(picked[j], early_turned[:, j])
         early_grouped = tile([P, 2 * P, PACK], BF16, "early_grouped")
         group_words(early_grouped[:], early_turned[:])
-        early_codes = reused.tile([P, 2 * P], U32, name="early_codes", align_bytes=64, offset=64)
+        early_codes = tile_at(64, [P, 2 * P], U32, "early_codes")
         early_scales = tile([P, 2 * P], U8, "early_scales")
         quantize(early_codes[:], early_scales[:], early_grouped[:])
 
         for h in range(HALVES):
-            r = inv_sum[:, h : h + 1]
-            w = tile([P, I], BF16, "w%d" % h)
-            nc.vector.scalar_tensor_tensor(w[:], probs[h][:], r, size_rows[:], ALU.mult, ALU.mult)
+            weights = tile([P, I], BF16, "weights%d" % h)
+            nc.vector.scalar_tensor_tensor(weights[:], probs[h][:], inv_sum[:, h : h + 1], size_rows[:], ALU.mult, ALU.mult)
             w_turned = bank(h, [P, 1, 2, P], "w_turned%d" % h)
-            turn_words(w, w_turned[:, 0])
-            group_words(w_grouped[:, P * h : P * (h + 1), :], w_turned[:])
+            turn_words(weights, w_turned[:, 0])
+            group_words(w_grouped[:, halves[h], :], w_turned[:])
 
         picked.append(gather_values(3))
-        late_codes = tile([P, Q + 2 * P], U32, "late_codes", "v_pool3")
+        late_codes = tile([P, Q + 2 * P], U32, "late_codes", instead_of="v_pool3")
         late_scales = tile([P, Q + 2 * P], U8, "late_scales")
         late_grouped = []
         for j in (2, 3):
@@ -172,34 +184,45 @@ def tile_attend_tokensharpness_pl_kernel(tc, query, keys_words, keys_scales, sha
             late_grouped.append(grouped)
         quantize(late_codes[:, 0:Q], late_scales[:, 0:Q], w_grouped[:])
         v_mx = [(early_codes[:, P * j : P * (j + 1)], early_scales[:, P * j : P * (j + 1)]) for j in range(2)]
-        for j in range(2):
-            cols = slice(Q + P * j, Q + P * (j + 1))
-            quantize(late_codes[:, cols], late_scales[:, cols], late_grouped[j][:])
+        for n, grouped in enumerate(late_grouped):
+            cols = slice(Q + P * n, Q + P * (n + 1))
+            quantize(late_codes[:, cols], late_scales[:, cols], grouped[:])
             v_mx.append((late_codes[:, cols], late_scales[:, cols]))
+
+        def product(j, n, queries):
+            result = bank(n, [P, queries.stop - queries.start], "result%d" % n)
+            nc.tensor.matmul_mx(
+                out=result[:],
+                lhsT=v_mx[j][0].bitcast(FP8X4),
+                lhsT_scale=v_mx[j][1],
+                rhs=late_codes[:, queries].bitcast(FP8X4),
+                rhs_scale=late_scales[:, queries],
+                start=True,
+                stop=True,
+            )
+            return result[:]
 
         y_f32 = tile([P, PACK, Q], F32, "y_f32")
         out_planes = out_0.rearrange("(m j) q -> m j q", j=PACK)
-        def product(j, n, cols):
-            y = bank(n, [P, cols.stop - cols.start], "y%d" % n)
-            nc.tensor.matmul_mx(out=y[:], lhsT=v_mx[j][0].bitcast(FP8X4), lhsT_scale=v_mx[j][1], rhs=late_codes[:, cols].bitcast(FP8X4), rhs_scale=late_scales[:, cols], start=True, stop=True)
-            return y
-
-        nc.scalar.copy(y_f32[:, 0, :], product(0, 2, slice(0, Q))[:])
-        nc.scalar.copy(y_f32[:, 1, :], product(1, 3, slice(0, Q))[:])
-        nc.vector.tensor_copy(y_f32[:, 2, :], product(2, 4, slice(0, Q))[:])
+        nc.scalar.copy(y_f32[:, 0, :], product(0, 2, slice(0, Q)))
+        nc.scalar.copy(y_f32[:, 1, :], product(1, 3, slice(0, Q)))
+        nc.vector.tensor_copy(y_f32[:, 2, :], product(2, 4, slice(0, Q)))
         nc.sync.dma_start(out_planes[:, 0:3, :], y_f32[:, 0:3, :])
-        nc.scalar.copy(y_f32[:, 3, halves[0]], product(3, 5, halves[0])[:])
-        nc.vector.tensor_copy(y_f32[:, 3, halves[1]], product(3, 6, halves[1])[:])
+        nc.scalar.copy(y_f32[:, 3, halves[0]], product(3, 5, halves[0]))
+        nc.vector.tensor_copy(y_f32[:, 3, halves[1]], product(3, 6, halves[1]))
         nc.scalar.dma_start(out_planes[:, 3, :], y_f32[:, 3, :])
 
         y_codes = tile([P, Q], U32, "y_codes")
         y_scales = tile([P, Q], U8, "y_scales")
-        y_bf = [tile([P, P, PACK], BF16, "y_bf%d" % h) for h in range(HALVES)]
+        y_grouped = [tile([P, P, PACK], BF16, "y_grouped%d" % h) for h in range(HALVES)]
         for h in range(HALVES):
-            nc.vector.tensor_copy(y_bf[h][:].rearrange("m (c i) j -> m c j i", i=4), y_f32[:, :, halves[h]].rearrange("m j (c i) -> m c j i", i=4))
+            nc.vector.tensor_copy(
+                y_grouped[h][:].rearrange("m (c i) j -> m c j i", i=LINE),
+                y_f32[:, :, halves[h]].rearrange("m j (c i) -> m c j i", i=LINE),
+            )
         for h in range(HALVES):
-            quantize(y_codes[:, halves[h]], y_scales[:, halves[h]], y_bf[h][:])
+            quantize(y_codes[:, halves[h]], y_scales[:, halves[h]], y_grouped[h][:])
         nc.sync.dma_start(out_1[0].rearrange("m q j -> m (q j)").bitcast(I32), y_codes[:].bitcast(I32))
-        for g in range(4):
+        for g in range(P // QUADRANT):
             queue = nc.sync if g % 2 == 0 else nc.scalar
-            queue.dma_start(out_2[0, 4 * g : 4 * g + 4, :].bitcast(I32), y_scales[32 * g : 32 * g + 4, :].bitcast(I32))
+            queue.dma_start(out_2[0, 4 * g : 4 * g + 4, :].bitcast(I32), y_scales[QUADRANT * g : QUADRANT * g + 4, :].bitcast(I32))

from contextlib import ExitStack

import concourse.mybir as mybir
from concourse.masks import make_identity

D, T, I, Q, E = 512, 2048, 512, 256, 512
FLOPS = 2 * D * Q * I + 2 * I * E * Q
BYTES = 4 * D * Q + D * T // 2 + D * T // 32 + 2 * 4 * T + 4 * I + 4 * E * T + 2 * 8 * I + 4 * E * Q + E * Q + E * Q // 32

F32 = mybir.dt.float32
BF16 = mybir.dt.bfloat16
I32 = mybir.dt.int32
U32 = mybir.dt.uint32
U16 = mybir.dt.uint16
U8 = mybir.dt.uint8
FP8X4 = mybir.dt.float8_e4m3fn_x4
FP4X4 = mybir.dt.float4_e2m1fn_x4
ACT = mybir.ActivationFunctionType
ALU = mybir.AluOpType
AX = mybir.AxisListType

P = 128
PACK = 4
QUADRANT = 32
LINE = 4
HALVES = Q // P
CHUNKS = I // P
ROW = P - 1


def tile_attend_tokensharpness_pl_kernel(tc, query, keys_words, keys_scales, sharp, tbias, size, vals, offs, out_0, out_1, out_2):
    nc = tc.nc
    with ExitStack() as ctx:
        lists = ctx.enter_context(tc.tile_pool(name="lists", bufs=1))
        sb = ctx.enter_context(tc.tile_pool(name="sb", bufs=1))
        reused = ctx.enter_context(tc.tile_pool(name="reused", bufs=1))
        ps = ctx.enter_context(tc.psum_pool(name="ps", bufs=1))

        def bank(n, shape, name):
            return ps.tile(shape, F32, name=name, tag="bank%d" % n)

        def tile(shape, dtype, name, instead_of=None):
            return sb.tile(shape, dtype, name=name, tag=instead_of or name, align_bytes=64)

        def tile_at(offset, shape, dtype, name):
            return reused.tile(shape, dtype, name=name, align_bytes=64, offset=offset)

        offsets = lists.tile([P, I // 16], U16, name="offsets")
        nc.sync.dma_start(offsets[:], offs)

        ks_pool = tile([P, T], U8, "ks_pool")
        sharp_pool = tile([P, T], F32, "sharp_pool")
        tbias_pool = tile([P, T], F32, "tbias_pool")
        nc.gpsimd.memset(ks_pool[:].bitcast(I32), 0)
        ident = tile([P, P], F32, "ident")
        nc.vector.memset(ident[:], 0.0)
        make_identity(nc, ident[:], nomemset=True)
        nc.vector.memset(sharp_pool[0:ROW, :], 0.0)
        nc.vector.memset(tbias_pool[0:ROW, :], 0.0)
        nc.sync.dma_start(sharp_pool[ROW:P, :], sharp[0:1, :])
        nc.sync.dma_start(tbias_pool[ROW:P, :], tbias[0:1, :])

        kw_pool = tile([P, T], U16, "kw_pool")
        nc.sync.dma_start(kw_pool[:].bitcast(I32), keys_words[0].bitcast(I32))
        q_raw = tile([P, PACK, Q], F32, "q_raw")
        nc.sync.dma_start(q_raw[:], query.rearrange("(p t) q -> p t q", t=PACK))
        size_cols = tile([P, PACK], F32, "size_cols")
        nc.sync.dma_start(size_cols[:], size.rearrange("o (p t) -> (o p) t", t=PACK))
        for r in range(4):
            nc.sync.dma_start(ks_pool[r:P:QUADRANT, :].bitcast(I32), keys_scales[0, r:16:4, :].bitcast(I32))
        vals_planes = vals.rearrange("(m j) t -> j m t", j=PACK)
        v_pool = [tile_at(0, [P, T], F32, "v_pool2") if j == 2 else tile([P, T], F32, "v_pool%d" % j) for j in range(PACK)]
        for j in range(PACK):
            nc.sync.dma_start(v_pool[j][:], vals_planes[j])

        kw = tile([P, I], U16, "kw")
        ks = tile([P, I], U8, "ks")

        q_grouped = tile([P, Q, PACK], BF16, "q_grouped")
        nc.scalar.activation(q_grouped[:].rearrange("p (c i) t -> p c t i", i=LINE), q_raw[:].rearrange("p t (c i) -> p c t i", i=LINE), ACT.Copy)
        q_codes = tile([P, Q], U32, "q_codes")
        q_scales = tile([P, Q], U8, "q_scales")

        size_rows = bank(6, [P, I], "size_rows")
        for t in range(PACK):
            nc.tensor.transpose(size_rows[:, t:I:PACK], size_cols[:, t : t + 1].to_broadcast([P, P]), ident[:])

        def listed_columns(window, n, name, instead_of=None):
            row = tile([P, I], F32, name + "_row")
            nc.vector.tensor_copy(row[:], window[:].indirect(offsets[:]))
            turned = bank(n, [P, CHUNKS, P], name + "_turned")
            for c in range(CHUNKS):
                nc.tensor.transpose(turned[:, c, :], row[:, P * c : P * (c + 1)], ident[:])
            cols = tile([P, CHUNKS], F32, name + "_cols", instead_of)
            nc.scalar.activation(cols[:], turned[:, :, ROW], ACT.Copy)
            return cols

        def gather_values(j):
            picked = tile([P, I], BF16, "v_picked%d" % j)
            nc.vector.tensor_copy(picked[:], v_pool[j][:].indirect(offsets[:]))
            return picked

        def turn_words(src, turned):
            words = src[:].bitcast(F32)
            for u in range(2):
                nc.tensor.transpose(turned[:, u, :], words[:, u : 2 * P : 2], ident[:])

        def group_words(grouped, turned):
            words = grouped.rearrange("p x t -> p (x t)").bitcast(F32)
            nc.scalar.copy(words.rearrange("p (n x u) -> p n x u", x=P, u=2), turned.rearrange("p n u x -> p n x u"))

        def quantize(codes, scales, grouped):
            nc.vector.quantize_mx(out=codes.bitcast(FP8X4), scales=scales, in_=grouped.rearrange("p x t -> p (x t)"))

        sharp_cols = listed_columns(sharp_pool, 4, "sharp", instead_of="q_raw")
        tbias_cols = listed_columns(tbias_pool, 5, "tbias")
        nc.vector.tensor_copy(kw[:], kw_pool[:].indirect(offsets[:]))
        nc.vector.tensor_copy(ks[:], ks_pool[:].indirect(offsets[:]))
        quantize(q_codes[:], q_scales[:], q_grouped[:])

        halves = [slice(P * h, P * (h + 1)) for h in range(HALVES)]
        first_scores = [bank(c, [P, P], "first_scores%d" % c) for c in range(CHUNKS)]
        second_scores = bank(7, [P, CHUNKS, P], "second_scores")
        scores = [[first_scores[c][:] for c in range(CHUNKS)], [second_scores[:, c, :] for c in range(CHUNKS)]]
        for h in range(HALVES):
            for c in range(CHUNKS):
                slots = slice(P * c, P * (c + 1))
                nc.tensor.matmul_mx(
                    out=scores[h][c],
                    lhsT=kw[:, slots].bitcast(FP4X4),
                    lhsT_scale=ks[:, slots],
                    rhs=q_codes[:, halves[h]].bitcast(FP8X4),
                    rhs_scale=q_scales[:, halves[h]],
                    start=True,
                    stop=True,
                )
        picked = [gather_values(j) for j in range(2)]
        logits = [bank(4 + h, [P, I], "logits%d" % h) for h in range(HALVES)]
        for h in range(HALVES):
            for c in range(CHUNKS):
                by_slot = tile([P, P], F32, "by_slot%d_%d" % (h, c))
                nc.scalar.activation(by_slot[:], scores[h][c], ACT.Identity, bias=tbias_cols[:, c : c + 1], scale=sharp_cols[:, c : c + 1])
                nc.tensor.transpose(logits[h][:, P * c : P * (c + 1)], by_slot[:], ident[:])

        probs = []
        sums = tile([P, HALVES], F32, "sums")
        neg_max = tile([P, HALVES], F32, "neg_max", instead_of="v_pool1")
        for h in range(HALVES):
            nc.vector.tensor_reduce(neg_max[:, h : h + 1], logits[h][:], AX.X, ALU.max, negate=True)
            prob = tile([P, I], F32, "probs%d" % h)
            nc.scalar.activation(prob[:], logits[h][:], ACT.Exp, bias=neg_max[:, h : h + 1], accum_out=sums[:, h : h + 1])
            probs.append(prob)
        picked.append(gather_values(2))

        w_grouped = tile([P, Q, PACK], BF16, "w_grouped")
        inv_sum = tile_at(0, [P, HALVES], F32, "inv_sum")
        nc.vector.reciprocal(inv_sum[:], sums[:])

        early_turned = bank(7, [P, 2, 2, P], "early_turned")
        for j in range(2):
            turn_words(picked[j], early_turned[:, j])
        early_grouped = tile([P, 2 * P, PACK], BF16, "early_grouped")
        group_words(early_grouped[:], early_turned[:])
        early_codes = tile_at(64, [P, 2 * P], U32, "early_codes")
        early_scales = tile([P, 2 * P], U8, "early_scales")
        quantize(early_codes[:], early_scales[:], early_grouped[:])

        for h in range(HALVES):
            weights = tile([P, I], BF16, "weights%d" % h)
            nc.vector.scalar_tensor_tensor(weights[:], probs[h][:], inv_sum[:, h : h + 1], size_rows[:], ALU.mult, ALU.mult)
            w_turned = bank(h, [P, 1, 2, P], "w_turned%d" % h)
            turn_words(weights, w_turned[:, 0])
            group_words(w_grouped[:, halves[h], :], w_turned[:])

        picked.append(gather_values(3))
        late_codes = tile([P, Q + 2 * P], U32, "late_codes", instead_of="v_pool3")
        late_scales = tile([P, Q + 2 * P], U8, "late_scales")
        late_grouped = []
        for j in (2, 3):
            late_turned = bank(7, [P, 1, 2, P], "late_turned%d" % j)
            turn_words(picked[j], late_turned[:, 0])
            grouped = tile([P, P, PACK], BF16, "late_grouped%d" % j)
            group_words(grouped[:], late_turned[:])
            late_grouped.append(grouped)
        quantize(late_codes[:, 0:Q], late_scales[:, 0:Q], w_grouped[:])
        v_mx = [(early_codes[:, P * j : P * (j + 1)], early_scales[:, P * j : P * (j + 1)]) for j in range(2)]
        for n, grouped in enumerate(late_grouped):
            cols = slice(Q + P * n, Q + P * (n + 1))
            quantize(late_codes[:, cols], late_scales[:, cols], grouped[:])
            v_mx.append((late_codes[:, cols], late_scales[:, cols]))

        def product(j, n, queries):
            result = bank(n, [P, queries.stop - queries.start], "result%d" % n)
            nc.tensor.matmul_mx(
                out=result[:],
                lhsT=v_mx[j][0].bitcast(FP8X4),
                lhsT_scale=v_mx[j][1],
                rhs=late_codes[:, queries].bitcast(FP8X4),
                rhs_scale=late_scales[:, queries],
                start=True,
                stop=True,
            )
            return result[:]

        y_f32 = tile([P, PACK, Q], F32, "y_f32")
        out_planes = out_0.rearrange("(m j) q -> m j q", j=PACK)
        nc.scalar.copy(y_f32[:, 0, :], product(0, 2, slice(0, Q)))
        nc.scalar.copy(y_f32[:, 1, :], product(1, 3, slice(0, Q)))
        nc.vector.tensor_copy(y_f32[:, 2, :], product(2, 4, slice(0, Q)))
        nc.sync.dma_start(out_planes[:, 0:3, :], y_f32[:, 0:3, :])
        nc.scalar.copy(y_f32[:, 3, halves[0]], product(3, 5, halves[0]))
        nc.vector.tensor_copy(y_f32[:, 3, halves[1]], product(3, 6, halves[1]))
        nc.scalar.dma_start(out_planes[:, 3, :], y_f32[:, 3, :])

        y_codes = tile([P, Q], U32, "y_codes")
        y_scales = tile([P, Q], U8, "y_scales")
        y_grouped = [tile([P, P, PACK], BF16, "y_grouped%d" % h) for h in range(HALVES)]
        for h in range(HALVES):
            nc.vector.tensor_copy(
                y_grouped[h][:].rearrange("m (c i) j -> m c j i", i=LINE),
                y_f32[:, :, halves[h]].rearrange("m j (c i) -> m c j i", i=LINE),
            )
        for h in range(HALVES):
            quantize(y_codes[:, halves[h]], y_scales[:, halves[h]], y_grouped[h][:])
        nc.sync.dma_start(out_1[0].rearrange("m q j -> m (q j)").bitcast(I32), y_codes[:].bitcast(I32))
        for g in range(P // QUADRANT):
            queue = nc.sync if g % 2 == 0 else nc.scalar
            queue.dma_start(out_2[0, 4 * g : 4 * g + 4, :].bitcast(I32), y_scales[QUADRANT * g : QUADRANT * g + 4, :].bitcast(I32))
